import numpy as np
import ml_dtypes


def mxq(x, axis, fmt="e4m3"):
    dtype, down = {"e4m3": (ml_dtypes.float8_e4m3fn, 7), "e5m2": (ml_dtypes.float8_e5m2, 14)}[fmt]
    v = np.moveaxis(np.asarray(x, np.float32).astype(ml_dtypes.bfloat16).astype(np.float64), axis, -1)
    blocks = v.reshape(v.shape[:-1] + (-1, 32))
    amax = np.abs(blocks).max(-1, keepdims=True)
    byte = np.maximum(np.where(amax > 0, np.frexp(amax)[1] - 1 + 127, 0) - down, 1)
    scale = np.exp2(byte - 127.0)
    codes = (blocks / scale).astype(np.float32).astype(dtype).astype(np.float64)
    return np.moveaxis((codes * scale).reshape(v.shape), -1, axis)


WIDE = False


def mx_kscale(k):
    if not WIDE:
        return np.ones(k)
    levels = np.array([10, -10, 5, -5, 0])
    if k % 512:
        return np.exp2(np.random.permutation(np.resize(levels, k // 32))).repeat(32)
    a = np.empty((k // 512, 16))
    for p in range(k // 512):
        a[p, :8] = np.random.permutation(np.resize(levels, 8))
        for g in range(8):
            far = levels[np.abs(levels - a[p, g]) >= 10]
            a[p, g + 8] = far[np.random.randint(len(far))]
    return np.exp2(a.ravel()).repeat(32)


def f64(x):
    return np.asarray(x).astype(np.float64)


def striped(idx):
    return np.tile(idx.reshape(-1, 16).T, (8, 1)).astype(np.uint16)


def unstriped(offs):
    return offs[:16].T.reshape(-1).astype(np.int64)


def striped8(idx):
    return np.concatenate([v.reshape(-1, 16).T for v in idx]).astype(np.uint16)


def unstriped8(offs):
    return np.stack([offs[16 * g:16 * g + 16].T.reshape(-1) for g in range(8)]).astype(np.int64)


E2M1 = np.array([0.0, 0.5, 1.0, 1.5, 2.0, 3.0, 4.0, 6.0, -0.0, -0.5, -1.0, -1.5, -2.0, -3.0, -4.0, -6.0])


def pack_weight(w, fmt):
    k, n = w.shape
    w = f64(np.asarray(w, np.float32).astype(ml_dtypes.bfloat16)).reshape(k // 32, 32, n)
    amax = np.abs(w).max(1)
    if fmt == "e4m3":
        byte = np.frexp(amax)[1] - 1 + 127 - 7
    else:
        mant, ex = np.frexp(amax / 6.0)
        byte = np.where(mant > 0.5, ex, ex - 1) + 127
    byte = np.clip(np.where(amax > 0, byte, 1), 1, 254)
    scaled = (w * np.exp2(127.0 - byte)[:, None, :]).reshape(k, n).astype(np.float32)
    by_word = np.ascontiguousarray(scaled.reshape(k // 512, 128, 4, n).transpose(0, 1, 3, 2))
    if fmt == "e4m3":
        words = by_word.astype(ml_dtypes.float8_e4m3fn).view(np.uint8)
    else:
        c = by_word.astype(ml_dtypes.float4_e2m1fn).view(np.uint8) & 0xF
        words = (c[..., 0::2] | (c[..., 1::2] << 4)).reshape(k // 512, 128, 2 * n)
    return np.ascontiguousarray(words), np.ascontiguousarray(byte.astype(np.uint8).reshape(k // 512, 16, n))


def unpack_weight(words, scales, fmt):
    g, _, n = scales.shape
    words = np.ascontiguousarray(words).reshape(g, 128, n, -1)
    if fmt == "e4m3":
        vals = words.view(ml_dtypes.float8_e4m3fn).astype(np.float64)
    else:
        nib = np.empty((g, 128, n, 4), np.uint8)
        nib[..., 0::2] = words & 0xF
        nib[..., 1::2] = words >> 4
        vals = E2M1[nib]
    vals = vals * np.repeat(np.exp2(scales.astype(np.float64) - 127.0), 8, axis=1)[..., None]
    return vals.transpose(0, 1, 3, 2).reshape(g * 512, n)


def pack_table(v):
    words, scales = pack_weight(v, "e4m3")
    return np.concatenate([words.reshape(words.shape[0], -1), scales.reshape(scales.shape[0], -1)], axis=1)


def unpack_table(tab):
    g, t = tab.shape[0], tab.shape[1] // 528
    return unpack_weight(tab[:, :512 * t].reshape(g, 128, t, 4), tab[:, 512 * t:].reshape(g, 16, t), "e4m3")


def silu(v):
    return v / (1.0 + np.exp(-np.maximum(v, -700.0)))


K, M, T, S = 1024, 1024, 512, 256


def setup_inputs():
    n = np.random.standard_normal
    s = mx_kscale(K)[:, None]
    return {
        "tab": pack_table(n((K, T)) * s),
        "w": (n((K, M)) / np.sqrt(K) / s).astype(np.float32),
        "b": (0.3 * n(1024)).astype(np.float32),
        "wgo": np.repeat(np.random.uniform(0.5, 2.0, (8, S)), 16, axis=0).astype(np.float32),
        "offs": striped(np.random.permutation(T)[:S]),
        "offs2": striped8(np.stack([np.random.permutation(T)[:S] for _ in range(8)])),
    }


def reference(tab, w, b, wgo, offs, offs2):
    tab_ = unpack_table(tab)[:, unstriped(offs)]
    w_ = mxq(f64(w), 0, "e4m3")
    y = w_.T @ tab_
    place = unstriped8(offs2)[np.arange(M) % 128 // 16]
    out = np.zeros((M, T))
    out[np.arange(M)[:, None], place] = f64(wgo)[np.arange(M) % 128] * (silu(y + f64(b)[:, None]))
    return out

@@ -1,0 +1,184 @@
+import concourse.mybir as mybir
+from concourse.masks import make_identity
+
+F32 = mybir.dt.float32
+BF16 = mybir.dt.bfloat16
+I32 = mybir.dt.int32
+U32 = mybir.dt.uint32
+U16 = mybir.dt.uint16
+U8 = mybir.dt.uint8
+FP8X4 = mybir.dt.float8_e4m3fn_x4
+MULT = mybir.AluOpType.mult
+SILU = mybir.ActivationFunctionType.Silu
+
+K, M, T, S = 1024, 1024, 512, 256
+FLOPS = 2 * K * M * S
+
+P = 128
+PASSES = K // 512
+TILES = M // P
+HALF = S // 2
+CHUNKS = ((0,), (1,), (2, 3), (4, 5), (6, 7))
+WINDOWS = 4
+
+
+def tile_list_tabhs_silu_kernel(tc, tab, w, b, wgo, offs, offs2, out):
+    nc = tc.nc
+    w_view = w.rearrange("(a p j) n -> a p j n", a=PASSES, j=4)
+    scale_rows = tab[:, 512 * T : 528 * T].rearrange("a (q t) -> a q t", q=16)
+
+    with (
+        tc.tile_pool(name="keep", bufs=1) as keep,
+        tc.psum_pool(name="sums", bufs=1) as psum,
+    ):
+        picks = keep.tile([P, S // 16], U16, name="picks")
+        places = keep.tile([P, S // 16], U16, name="places")
+        planes = keep.tile([P, T], U8, name="planes", align_bytes=64)
+        words = [keep.tile([P, T], I32, name=f"words{a}", align_bytes=64) for a in range(PASSES)]
+        got_words = [keep.tile([P, S], U32, name=f"got_words{a}", align_bytes=64) for a in range(PASSES)]
+        got_planes = keep.tile([P, S], U8, name="got_planes", align_bytes=64)
+        factors = keep.tile([P, S], F32, name="factors")
+        bias_rows = keep.tile([P, P], F32, name="bias_rows")
+        ident = keep.tile([P, P], F32, name="ident")
+        bias = keep.tile([P, TILES], F32, name="bias")
+        dummy = keep.tile([P, 8], F32, name="dummy")
+        windows = [keep.tile([P, T], F32, name=f"window{i}") for i in range(WINDOWS)]
+        raw, grouped, codes, scales = {}, {}, {}, {}
+        for c, chunk in enumerate(CHUNKS):
+            n = P * len(chunk)
+            for a in range(PASSES):
+                raw[c, a] = keep.tile([P, 4, n], F32, name=f"raw{c}_{a}")
+            grouped[c] = keep.tile([P, 8 * n], BF16, name=f"grouped{c}", align_bytes=64)
+            codes[c] = keep.tile([P, 2 * n], U32, name=f"codes{c}", align_bytes=64)
+            scales[c] = keep.tile([P, 2 * n], U8, name=f"scales{c}", align_bytes=64)
+
+        def load_w(c, a):
+            c0, n = P * CHUNKS[c][0], P * len(CHUNKS[c])
+            nc.sync.dma_start(out=raw[c, a][:], in_=w_view[a, :, :, c0 : c0 + n])
+
+        nc.gpsimd.memset(planes[:].bitcast(I32), 0)
+        nc.sync.dma_start(picks[:], offs)
+
+        def load_words(a):
+            nc.sync.dma_start(
+                out=words[a][:],
+                in_=tab[a, 0 : 512 * T].rearrange("(p x) -> p x", p=P).bitcast(I32),
+            )
+
+        load_words(0)
+        for q in range(4):
+            nc.sync.dma_start(
+                out=planes[32 * q : 32 * q + 8, :].bitcast(I32),
+                in_=scale_rows[:, 4 * q : 4 * q + 4, :].bitcast(I32),
+            )
+        nc.vector.memset(bias_rows[:], 0.0)
+        nc.sync.dma_start(out=bias_rows[0:TILES, :], in_=b.rearrange("(c p) -> c p", p=P))
+        load_words(1)
+        for a in range(PASSES):
+            load_w(0, a)
+        nc.vector.memset(dummy[:], 0.0)
+        nc.scalar.activation(out=dummy[:, 1:2], in_=dummy[:, 0:1], func=SILU)
+        make_identity(nc, ident[:])
+        for window in windows:
+            nc.vector.memset(window[:], 0.0)
+        for a in range(PASSES):
+            load_w(1, a)
+        nc.sync.dma_start(places[:], offs2)
+        nc.sync.dma_start(out=factors[:], in_=wgo)
+        for c in range(2, len(CHUNKS)):
+            for a in range(PASSES):
+                load_w(c, a)
+
+        def gather(h):
+            cols = slice(HALF * h, HALF * h + HALF)
+            lst = picks[:, 8 * h : 8 * h + 8]
+            for a in range(PASSES):
+                nc.vector.tensor_copy(got_words[a][:, cols], words[a][:].bitcast(U32).indirect(lst))
+            nc.vector.tensor_copy(got_planes[:, cols], planes[:].indirect(lst))
+
+        def interleave(engine_copy, c, i, a, lo=0, hi=P):
+            base = 1024 * i + 512 * a
+            engine_copy(
+                out=grouped[c][:, base + 4 * lo : base + 4 * hi].rearrange("p (c i t) -> p c t i", i=4, t=4),
+                in_=raw[c, a][:, :, P * i + lo : P * i + hi].rearrange("p t (c i) -> p c t i", i=4),
+            )
+
+        def quantize(c, lo, hi):
+            nc.vector.quantize_mx(
+                out=codes[c][:, lo // 4 : hi // 4].bitcast(FP8X4),
+                scales=scales[c][:, lo // 4 : hi // 4],
+                in_=grouped[c][:, lo:hi],
+            )
+
+        def multiply(acc, c, i, lo, hi):
+            for a in range(PASSES):
+                cols = slice(2 * P * i + P * a, 2 * P * i + P * a + P)
+                nc.tensor.matmul_mx(
+                    out=acc[:],
+                    lhsT=codes[c][:, cols].bitcast(FP8X4),
+                    lhsT_scale=scales[c][:, cols],
+                    rhs=got_words[a][:, lo:hi].bitcast(FP8X4),
+                    rhs_scale=got_planes[4 * a : P, lo:hi],
+                    start=(a == 0),
+                    stop=(a == PASSES - 1),
+                )
+
+        acts = [keep.tile([P, S], F32, name=f"act{m}") for m in range(TILES)]
+
+        def activate(acc, m, lo, hi):
+            nc.scalar.activation(out=acts[m][:, lo:hi], in_=acc[:], func=SILU, bias=bias[:, m : m + 1])
+
+        def scatter(m, h):
+            cols = slice(HALF * h, HALF * h + HALF)
+            nc.vector.tensor_tensor(
+                windows[m % WINDOWS][:].indirect(places[:, 8 * h : 8 * h + 8]),
+                acts[m][:, cols],
+                factors[:, cols],
+                MULT,
+            )
+
+        def store(m):
+            nc.sync.dma_start(out=out[P * m : P * m + P, :], in_=windows[m % WINDOWS][:])
+
+        def project(c, i):
+            acc = psum.tile([P, S], F32, name="acc", bufs=5)
+            multiply(acc, c, i, 0, S)
+            activate(acc, CHUNKS[c][i], 0, S)
+
+        gather(0)
+        interleave(nc.scalar.copy, 0, 0, 0)
+        quantize(0, 0, 512)
+        interleave(nc.vector.tensor_copy, 0, 0, 1, 0, 64)
+        interleave(nc.scalar.copy, 0, 0, 1, 64, P)
+        quantize(0, 512, 1024)
+        gather(1)
+        bias_t = psum.tile([P, P], F32, name="bias_t")
+        nc.tensor.transpose(bias_t[:], bias_rows[:], ident[:])
+        nc.scalar.copy(out=bias[:], in_=bias_t[:, 0:TILES])
+        for h in range(2):
+            part = psum.tile([P, HALF], F32, name="part", bufs=2)
+            multiply(part, 0, 0, HALF * h, HALF * h + HALF)
+            activate(part, 0, HALF * h, HALF * h + HALF)
+
+        where = {m: (c, i) for c, chunk in enumerate(CHUNKS) for i, m in enumerate(chunk)}
+
+        def prepare(m):
+            if m < TILES:
+                c, i = where[m]
+                for a in range(PASSES):
+                    interleave(nc.scalar.copy, c, i, a)
+                quantize(c, 1024 * i, 1024 * i + 1024)
+                project(c, i)
+
+        prepare(1)
+        scatter(0, 0)
+        prepare(2)
+        scatter(0, 1)
+        store(0)
+        scatter(1, 0)
+        for m in range(1, TILES):
+            prepare(m + 2)
+            if m + 1 < TILES:
+                scatter(m + 1, 0)
+            scatter(m, 1)
+            store(m)

@@ -34,7 +34,7 @@ def tile_list_tabhs_silu_kernel(tc, tab, w, b, wgo, offs, offs2, out):
         picks = keep.tile([P, S // 16], U16, name="picks")
         places = keep.tile([P, S // 16], U16, name="places")
         planes = keep.tile([P, T], U8, name="planes", align_bytes=64)
-        words = [keep.tile([P, T], I32, name=f"words{a}", align_bytes=64) for a in range(PASSES)]
+        words = keep.tile([P, PASSES, T], I32, name="words", align_bytes=64)
         got_words = [keep.tile([P, S], U32, name=f"got_words{a}", align_bytes=64) for a in range(PASSES)]
         got_planes = keep.tile([P, S], U8, name="got_planes", align_bytes=64)
         factors = keep.tile([P, S], F32, name="factors")
@@ -57,30 +57,25 @@ def tile_list_tabhs_silu_kernel(tc, tab, w, b, wgo, offs, offs2, out):
             nc.sync.dma_start(out=raw[c, a][:], in_=w_view[a, :, :, c0 : c0 + n])
 
         nc.gpsimd.memset(planes[:].bitcast(I32), 0)
+        nc.vector.memset(bias_rows[:], 0.0)
+        nc.vector.memset(dummy[:], 0.0)
         nc.sync.dma_start(picks[:], offs)
-
-        def load_words(a):
-            nc.sync.dma_start(
-                out=words[a][:],
-                in_=tab[a, 0 : 512 * T].rearrange("(p x) -> p x", p=P).bitcast(I32),
-            )
-
-        load_words(0)
         for q in range(4):
             nc.sync.dma_start(
                 out=planes[32 * q : 32 * q + 8, :].bitcast(I32),
                 in_=scale_rows[:, 4 * q : 4 * q + 4, :].bitcast(I32),
             )
-        nc.vector.memset(bias_rows[:], 0.0)
-        nc.sync.dma_start(out=bias_rows[0:TILES, :], in_=b.rearrange("(c p) -> c p", p=P))
-        load_words(1)
+        nc.sync.dma_start(
+            out=words[:],
+            in_=tab[:, 0 : 512 * T].rearrange("a (p x) -> p a x", p=P).bitcast(I32),
+        )
         for a in range(PASSES):
             load_w(0, a)
-        nc.vector.memset(dummy[:], 0.0)
         nc.scalar.activation(out=dummy[:, 1:2], in_=dummy[:, 0:1], func=SILU)
         make_identity(nc, ident[:])
         for window in windows:
             nc.vector.memset(window[:], 0.0)
+        nc.sync.dma_start(out=bias_rows[0:TILES, :], in_=b.rearrange("(c p) -> c p", p=P))
         for a in range(PASSES):
             load_w(1, a)
         nc.sync.dma_start(places[:], offs2)
@@ -93,7 +88,7 @@ def tile_list_tabhs_silu_kernel(tc, tab, w, b, wgo, offs, offs2, out):
             cols = slice(HALF * h, HALF * h + HALF)
             lst = picks[:, 8 * h : 8 * h + 8]
             for a in range(PASSES):
-                nc.vector.tensor_copy(got_words[a][:, cols], words[a][:].bitcast(U32).indirect(lst))
+                nc.vector.tensor_copy(got_words[a][:, cols], words[:, a, :].bitcast(U32).indirect(lst))
             nc.vector.tensor_copy(got_planes[:, cols], planes[:].indirect(lst))
 
         def interleave(engine_copy, c, i, a, lo=0, hi=P):
@@ -123,16 +118,24 @@ def tile_list_tabhs_silu_kernel(tc, tab, w, b, wgo, offs, offs2, out):
                     stop=(a == PASSES - 1),
                 )
 
-        acts = [keep.tile([P, S], F32, name=f"act{m}") for m in range(TILES)]
+        where = {m: (c, i) for c, chunk in enumerate(CHUNKS) for i, m in enumerate(chunk)}
+        spare = keep.tile([P, 4, HALF], F32, name="spare")
+        homes = {(0, 0): spare[:, 0, :], (6, 1): spare[:, 1, :], (7, 0): spare[:, 2, :], (7, 1): spare[:, 3, :]}
+        for m in range(TILES):
+            for h in range(2):
+                if (m, h) not in homes:
+                    t, s = (1, 0) if m == 0 else (m + 1 + h, h)
+                    c, i = where[t]
+                    homes[m, h] = raw[c, 1][:, s, P * i : P * i + P]
 
-        def activate(acc, m, lo, hi):
-            nc.scalar.activation(out=acts[m][:, lo:hi], in_=acc[:], func=SILU, bias=bias[:, m : m + 1])
+        def activate(acc, m, h):
+            nc.scalar.activation(out=homes[m, h], in_=acc, func=SILU, bias=bias[:, m : m + 1])
 
         def scatter(m, h):
             cols = slice(HALF * h, HALF * h + HALF)
             nc.vector.tensor_tensor(
                 windows[m % WINDOWS][:].indirect(places[:, 8 * h : 8 * h + 8]),
-                acts[m][:, cols],
+                homes[m, h],
                 factors[:, cols],
                 MULT,
             )
@@ -140,44 +143,56 @@ def tile_list_tabhs_silu_kernel(tc, tab, w, b, wgo, offs, offs2, out):
         def store(m):
             nc.sync.dma_start(out=out[P * m : P * m + P, :], in_=windows[m % WINDOWS][:])
 
-        def project(c, i):
-            acc = psum.tile([P, S], F32, name="acc", bufs=5)
-            multiply(acc, c, i, 0, S)
-            activate(acc, CHUNKS[c][i], 0, S)
-
         gather(0)
         interleave(nc.scalar.copy, 0, 0, 0)
         quantize(0, 0, 512)
         interleave(nc.vector.tensor_copy, 0, 0, 1, 0, 64)
         interleave(nc.scalar.copy, 0, 0, 1, 64, P)
         quantize(0, 512, 1024)
-        gather(1)
         bias_t = psum.tile([P, P], F32, name="bias_t")
         nc.tensor.transpose(bias_t[:], bias_rows[:], ident[:])
-        nc.scalar.copy(out=bias[:], in_=bias_t[:, 0:TILES])
-        for h in range(2):
+        nc.vector.tensor_copy(out=bias[:], in_=bias_t[:, 0:TILES])
+
+        def project_half(h):
             part = psum.tile([P, HALF], F32, name="part", bufs=2)
             multiply(part, 0, 0, HALF * h, HALF * h + HALF)
-            activate(part, 0, HALF * h, HALF * h + HALF)
+            activate(part[:], 0, h)
 
-        where = {m: (c, i) for c, chunk in enumerate(CHUNKS) for i, m in enumerate(chunk)}
-
-        def prepare(m):
+        def arrange(m):
             if m < TILES:
                 c, i = where[m]
                 for a in range(PASSES):
                     interleave(nc.scalar.copy, c, i, a)
-                quantize(c, 1024 * i, 1024 * i + 1024)
-                project(c, i)
 
-        prepare(1)
+        def finish(m):
+            if m < TILES:
+                c, i = where[m]
+                quantize(c, 1024 * i, 1024 * i + 1024)
+                accs[m] = psum.tile([P, S], F32, name="acc", bufs=5)
+                multiply(accs[m], c, i, 0, S)
+
+        accs = {}
+
+        def half(m, h):
+            activate(accs[m][:, HALF * h : HALF * h + HALF], m, h)
+
+        project_half(0)
+        gather(1)
+        arrange(1)
+        project_half(1)
         scatter(0, 0)
-        prepare(2)
+        arrange(2)
+        finish(1)
+        half(1, 0)
         scatter(0, 1)
         store(0)
         scatter(1, 0)
         for m in range(1, TILES):
-            prepare(m + 2)
+            arrange(m + 2)
+            finish(m + 1)
+            if m + 1 < TILES:
+                half(m + 1, 0)
+            half(m, 1)
             if m + 1 < TILES:
                 scatter(m + 1, 0)
             scatter(m, 1)

@@ -18,7 +18,7 @@ P = 128
 PASSES = K // 512
 TILES = M // P
 HALF = S // 2
-CHUNKS = ((0,), (1,), (2, 3), (4, 5), (6, 7))
+CHUNKS = ((0,), (1,), (2,), (3,), (4, 5), (6, 7))
 WINDOWS = 4
 
 
@@ -60,21 +60,21 @@ def tile_list_tabhs_silu_kernel(tc, tab, w, b, wgo, offs, offs2, out):
         nc.vector.memset(bias_rows[:], 0.0)
         nc.vector.memset(dummy[:], 0.0)
         nc.sync.dma_start(picks[:], offs)
+        nc.sync.dma_start(
+            out=words[:],
+            in_=tab[:, 0 : 512 * T].rearrange("a (p x) -> p a x", p=P).bitcast(I32),
+        )
         for q in range(4):
             nc.sync.dma_start(
                 out=planes[32 * q : 32 * q + 8, :].bitcast(I32),
                 in_=scale_rows[:, 4 * q : 4 * q + 4, :].bitcast(I32),
             )
-        nc.sync.dma_start(
-            out=words[:],
-            in_=tab[:, 0 : 512 * T].rearrange("a (p x) -> p a x", p=P).bitcast(I32),
-        )
         for a in range(PASSES):
             load_w(0, a)
         nc.scalar.activation(out=dummy[:, 1:2], in_=dummy[:, 0:1], func=SILU)
         make_identity(nc, ident[:])
-        for window in windows:
-            nc.vector.memset(window[:], 0.0)
+        for i, window in enumerate(windows):
+            (nc.vector if i < 2 else nc.gpsimd).memset(window[:], 0.0)
         nc.sync.dma_start(out=bias_rows[0:TILES, :], in_=b.rearrange("(c p) -> c p", p=P))
         for a in range(PASSES):
             load_w(1, a)

@@ -18,7 +18,7 @@ P = 128
 PASSES = K // 512
 TILES = M // P
 HALF = S // 2
-CHUNKS = ((0,), (1,), (2,), (3,), (4, 5), (6, 7))
+CHUNKS = ((0,), (1,), (2,), (3,), (4,), (5, 6), (7,))
 WINDOWS = 4
 
 
@@ -76,10 +76,10 @@ def tile_list_tabhs_silu_kernel(tc, tab, w, b, wgo, offs, offs2, out):
         for i, window in enumerate(windows):
             (nc.vector if i < 2 else nc.gpsimd).memset(window[:], 0.0)
         nc.sync.dma_start(out=bias_rows[0:TILES, :], in_=b.rearrange("(c p) -> c p", p=P))
+        nc.sync.dma_start(places[:], offs2)
         for a in range(PASSES):
             load_w(1, a)
-        nc.sync.dma_start(places[:], offs2)
-        nc.sync.dma_start(out=factors[:], in_=wgo)
+            nc.sync.dma_start(out=factors[:, HALF * a : HALF * a + HALF], in_=wgo[:, HALF * a : HALF * a + HALF])
         for c in range(2, len(CHUNKS)):
             for a in range(PASSES):
                 load_w(c, a)

import concourse.mybir as mybir
from concourse.masks import make_identity

F32 = mybir.dt.float32
BF16 = mybir.dt.bfloat16
I32 = mybir.dt.int32
U32 = mybir.dt.uint32
U16 = mybir.dt.uint16
U8 = mybir.dt.uint8
FP8X4 = mybir.dt.float8_e4m3fn_x4
MULT = mybir.AluOpType.mult
SILU = mybir.ActivationFunctionType.Silu

K, M, T, S = 1024, 1024, 512, 256
FLOPS = 2 * K * M * S

P = 128
PASSES = K // 512
TILES = M // P
HALF = S // 2
CHUNKS = ((0,), (1,), (2,), (3,), (4,), (5, 6), (7,))
WINDOWS = 4


def tile_list_tabhs_silu_kernel(tc, tab, w, b, wgo, offs, offs2, out):
    nc = tc.nc
    w_view = w.rearrange("(a p j) n -> a p j n", a=PASSES, j=4)
    scale_rows = tab[:, 512 * T : 528 * T].rearrange("a (q t) -> a q t", q=16)

    with (
        tc.tile_pool(name="keep", bufs=1) as keep,
        tc.psum_pool(name="sums", bufs=1) as psum,
    ):
        picks = keep.tile([P, S // 16], U16, name="picks")
        places = keep.tile([P, S // 16], U16, name="places")
        planes = keep.tile([P, T], U8, name="planes", align_bytes=64)
        words = keep.tile([P, PASSES, T], I32, name="words", align_bytes=64)
        got_words = [keep.tile([P, S], U32, name=f"got_words{a}", align_bytes=64) for a in range(PASSES)]
        got_planes = keep.tile([P, S], U8, name="got_planes", align_bytes=64)
        factors = keep.tile([P, S], F32, name="factors")
        bias_rows = keep.tile([P, P], F32, name="bias_rows")
        ident = keep.tile([P, P], F32, name="ident")
        bias = keep.tile([P, TILES], F32, name="bias")
        dummy = keep.tile([P, 8], F32, name="dummy")
        windows = [keep.tile([P, T], F32, name=f"window{i}") for i in range(WINDOWS)]
        raw, grouped, codes, scales = {}, {}, {}, {}
        for c, chunk in enumerate(CHUNKS):
            n = P * len(chunk)
            for a in range(PASSES):
                raw[c, a] = keep.tile([P, 4, n], F32, name=f"raw{c}_{a}")
            grouped[c] = keep.tile([P, 8 * n], BF16, name=f"grouped{c}", align_bytes=64)
            codes[c] = keep.tile([P, 2 * n], U32, name=f"codes{c}", align_bytes=64)
            scales[c] = keep.tile([P, 2 * n], U8, name=f"scales{c}", align_bytes=64)

        def load_w(c, a):
            c0, n = P * CHUNKS[c][0], P * len(CHUNKS[c])
            nc.sync.dma_start(out=raw[c, a][:], in_=w_view[a, :, :, c0 : c0 + n])

        nc.gpsimd.memset(planes[:].bitcast(I32), 0)
        nc.vector.memset(bias_rows[:], 0.0)
        nc.vector.memset(dummy[:], 0.0)
        nc.sync.dma_start(picks[:], offs)
        nc.sync.dma_start(
            out=words[:],
            in_=tab[:, 0 : 512 * T].rearrange("a (p x) -> p a x", p=P).bitcast(I32),
        )
        for q in range(4):
            nc.sync.dma_start(
                out=planes[32 * q : 32 * q + 8, :].bitcast(I32),
                in_=scale_rows[:, 4 * q : 4 * q + 4, :].bitcast(I32),
            )
        for a in range(PASSES):
            load_w(0, a)
        nc.scalar.activation(out=dummy[:, 1:2], in_=dummy[:, 0:1], func=SILU)
        make_identity(nc, ident[:])
        for i, window in enumerate(windows):
            (nc.vector if i < 2 else nc.gpsimd).memset(window[:], 0.0)
        nc.sync.dma_start(out=bias_rows[0:TILES, :], in_=b.rearrange("(c p) -> c p", p=P))
        nc.sync.dma_start(places[:], offs2)
        for a in range(PASSES):
            load_w(1, a)
            nc.sync.dma_start(out=factors[:, HALF * a : HALF * a + HALF], in_=wgo[:, HALF * a : HALF * a + HALF])
        for c in range(2, len(CHUNKS)):
            for a in range(PASSES):
                load_w(c, a)

        def gather(h):
            cols = slice(HALF * h, HALF * h + HALF)
            lst = picks[:, 8 * h : 8 * h + 8]
            for a in range(PASSES):
                nc.vector.tensor_copy(got_words[a][:, cols], words[:, a, :].bitcast(U32).indirect(lst))
            nc.vector.tensor_copy(got_planes[:, cols], planes[:].indirect(lst))

        def interleave(engine_copy, c, i, a, lo=0, hi=P):
            base = 1024 * i + 512 * a
            engine_copy(
                out=grouped[c][:, base + 4 * lo : base + 4 * hi].rearrange("p (c i t) -> p c t i", i=4, t=4),
                in_=raw[c, a][:, :, P * i + lo : P * i + hi].rearrange("p t (c i) -> p c t i", i=4),
            )

        def quantize(c, lo, hi):
            nc.vector.quantize_mx(
                out=codes[c][:, lo // 4 : hi // 4].bitcast(FP8X4),
                scales=scales[c][:, lo // 4 : hi // 4],
                in_=grouped[c][:, lo:hi],
            )

        def multiply(acc, c, i, lo, hi):
            for a in range(PASSES):
                cols = slice(2 * P * i + P * a, 2 * P * i + P * a + P)
                nc.tensor.matmul_mx(
                    out=acc[:],
                    lhsT=codes[c][:, cols].bitcast(FP8X4),
                    lhsT_scale=scales[c][:, cols],
                    rhs=got_words[a][:, lo:hi].bitcast(FP8X4),
                    rhs_scale=got_planes[4 * a : P, lo:hi],
                    start=(a == 0),
                    stop=(a == PASSES - 1),
                )

        where = {m: (c, i) for c, chunk in enumerate(CHUNKS) for i, m in enumerate(chunk)}
        spare = keep.tile([P, 4, HALF], F32, name="spare")
        homes = {(0, 0): spare[:, 0, :], (6, 1): spare[:, 1, :], (7, 0): spare[:, 2, :], (7, 1): spare[:, 3, :]}
        for m in range(TILES):
            for h in range(2):
                if (m, h) not in homes:
                    t, s = (1, 0) if m == 0 else (m + 1 + h, h)
                    c, i = where[t]
                    homes[m, h] = raw[c, 1][:, s, P * i : P * i + P]

        def activate(acc, m, h):
            nc.scalar.activation(out=homes[m, h], in_=acc, func=SILU, bias=bias[:, m : m + 1])

        def scatter(m, h):
            cols = slice(HALF * h, HALF * h + HALF)
            nc.vector.tensor_tensor(
                windows[m % WINDOWS][:].indirect(places[:, 8 * h : 8 * h + 8]),
                homes[m, h],
                factors[:, cols],
                MULT,
            )

        def store(m):
            nc.sync.dma_start(out=out[P * m : P * m + P, :], in_=windows[m % WINDOWS][:])

        gather(0)
        interleave(nc.scalar.copy, 0, 0, 0)
        quantize(0, 0, 512)
        interleave(nc.vector.tensor_copy, 0, 0, 1, 0, 64)
        interleave(nc.scalar.copy, 0, 0, 1, 64, P)
        quantize(0, 512, 1024)
        bias_t = psum.tile([P, P], F32, name="bias_t")
        nc.tensor.transpose(bias_t[:], bias_rows[:], ident[:])
        nc.vector.tensor_copy(out=bias[:], in_=bias_t[:, 0:TILES])

        def project_half(h):
            part = psum.tile([P, HALF], F32, name="part", bufs=2)
            multiply(part, 0, 0, HALF * h, HALF * h + HALF)
            activate(part[:], 0, h)

        def arrange(m):
            if m < TILES:
                c, i = where[m]
                for a in range(PASSES):
                    interleave(nc.scalar.copy, c, i, a)

        def finish(m):
            if m < TILES:
                c, i = where[m]
                quantize(c, 1024 * i, 1024 * i + 1024)
                accs[m] = psum.tile([P, S], F32, name="acc", bufs=5)
                multiply(accs[m], c, i, 0, S)

        accs = {}

        def half(m, h):
            activate(accs[m][:, HALF * h : HALF * h + HALF], m, h)

        project_half(0)
        gather(1)
        arrange(1)
        project_half(1)
        scatter(0, 0)
        arrange(2)
        finish(1)
        half(1, 0)
        scatter(0, 1)
        store(0)
        scatter(1, 0)
        for m in range(1, TILES):
            arrange(m + 2)
            finish(m + 1)
            if m + 1 < TILES:
                half(m + 1, 0)
            half(m, 1)
            if m + 1 < TILES:
                scatter(m + 1, 0)
            scatter(m, 1)
            store(m)
